import numpy as np
import ml_dtypes


def mxq(x, axis, fmt="e4m3"):
    dtype, down = {"e4m3": (ml_dtypes.float8_e4m3fn, 7), "e5m2": (ml_dtypes.float8_e5m2, 14)}[fmt]
    v = np.moveaxis(np.asarray(x, np.float32).astype(ml_dtypes.bfloat16).astype(np.float64), axis, -1)
    blocks = v.reshape(v.shape[:-1] + (-1, 32))
    amax = np.abs(blocks).max(-1, keepdims=True)
    byte = np.maximum(np.where(amax > 0, np.frexp(amax)[1] - 1 + 127, 0) - down, 1)
    scale = np.exp2(byte - 127.0)
    codes = (blocks / scale).astype(np.float32).astype(dtype).astype(np.float64)
    return np.moveaxis((codes * scale).reshape(v.shape), -1, axis)


WIDE = False


def mx_kscale(k):
    if not WIDE:
        return np.ones(k)
    levels = np.array([10, -10, 5, -5, 0])
    if k % 512:
        return np.exp2(np.random.permutation(np.resize(levels, k // 32))).repeat(32)
    a = np.empty((k // 512, 16))
    for p in range(k // 512):
        a[p, :8] = np.random.permutation(np.resize(levels, 8))
        for g in range(8):
            far = levels[np.abs(levels - a[p, g]) >= 10]
            a[p, g + 8] = far[np.random.randint(len(far))]
    return np.exp2(a.ravel()).repeat(32)


def f64(x):
    return np.asarray(x).astype(np.float64)


def striped(idx):
    return np.tile(idx.reshape(-1, 16).T, (8, 1)).astype(np.uint16)


def unstriped(offs):
    return offs[:16].T.reshape(-1).astype(np.int64)


def striped8(idx):
    return np.concatenate([x.reshape(-1, 16).T for x in idx]).astype(np.uint16)


def runs(offs, k):
    lists = np.stack([offs[16 * r : 16 * r + 16].T.reshape(-1) for r in range(8)]).astype(np.int64)
    return lists[np.arange(k) % 512 // 64]


def pack_weight(w):
    k, n = w.shape
    w = f64(np.asarray(w, np.float32).astype(ml_dtypes.bfloat16)).reshape(k // 32, 32, n)
    amax = np.abs(w).max(1)
    byte = np.clip(np.where(amax > 0, np.frexp(amax)[1] - 1 + 127 - 7, 1), 1, 254)
    scaled = (w * np.exp2(127.0 - byte)[:, None, :]).reshape(k, n).astype(np.float32)
    words = np.ascontiguousarray(scaled.reshape(k // 512, 128, 4, n).transpose(0, 1, 3, 2)).astype(ml_dtypes.float8_e4m3fn).view(np.uint8)
    return words, np.ascontiguousarray(byte.astype(np.uint8).reshape(k // 512, 16, n))


def unpack_weight(words, scales):
    g, p, n, _ = words.shape
    vals = np.ascontiguousarray(words).view(ml_dtypes.float8_e4m3fn).astype(np.float64) * np.repeat(np.exp2(scales.astype(np.float64) - 127.0), 8, axis=1)[..., None]
    return vals.transpose(0, 1, 3, 2).reshape(g * 512, n)


K, T, S, H, C = 512, 2048, 256, 512, 512


def setup_inputs():
    n = np.random.standard_normal
    s = mx_kscale(K)[:, None]
    packed_xT = pack_weight(n((K, T)) * s)
    return {
        "x_words": packed_xT[0],
        "x_scales": packed_xT[1],
        "w1": (n((K, H)) / np.sqrt(K) / s).astype(np.float32),
        "gs": (np.random.uniform(0.5, 1.5, (K, 1)) / s).astype(np.float32),
        "offs": striped(np.random.permutation(T)[:S]),
        "n1": striped8(np.stack([np.random.permutation(S) for _ in range(8)])),
        "n2": striped8(np.stack([np.random.permutation(S) for _ in range(8)])),
        "ca": striped(np.random.permutation(T)[:C]),
        "hc": striped8(np.random.randint(0, T, (8, C))),
        "n3": striped8(np.stack([np.random.permutation(S) for _ in range(8)])),
        "n4": striped8(np.stack([np.random.permutation(S) for _ in range(8)])),
        "n5": striped8(np.stack([np.random.permutation(S) for _ in range(8)])),
        "n6": striped8(np.stack([np.random.permutation(S) for _ in range(8)])),
    }


def reference(x_words, x_scales, w1, gs, offs, n1, n2, ca, hc, n3, n4, n5, n6):
    x_ca = unpack_weight(x_words, x_scales)[:, unstriped(ca)]
    xq = unpack_weight(x_words, x_scales)[:, unstriped(offs)]
    y = mxq(f64(w1), 0, "e4m3").T @ xq
    z = f64(gs) * (y[np.arange(H)[:, None], runs(n1, H)] + 0.75 * (y[np.arange(H)[:, None], runs(n2, H)]))
    zq = mxq(z, 0, "e4m3")
    a = 0.0625 * (x_ca.T @ zq)
    x_hc = unpack_weight(x_words, x_scales)[np.arange(K)[:, None], runs(hc, K)]
    b = 0.0625 * (x_hc.T @ zq)
    return np.maximum(a[np.arange(C)[:, None], runs(n3, C)] + b[np.arange(C)[:, None], runs(n5, C)], a[np.arange(C)[:, None], runs(n4, C)] + b[np.arange(C)[:, None], runs(n6, C)])

@@ -1,0 +1,193 @@
+from contextlib import ExitStack
+
+import concourse.mybir as mybir
+
+K, T, S, H, C = 512, 2048, 256, 512, 512
+FLOPS = 2 * K * H * S + 2 * 2 * K * C * S
+
+F32 = mybir.dt.float32
+BF16 = mybir.dt.bfloat16
+I32 = mybir.dt.int32
+U32 = mybir.dt.uint32
+U16 = mybir.dt.uint16
+U8 = mybir.dt.uint8
+FP8X4 = mybir.dt.float8_e4m3fn_x4
+COPY = mybir.ActivationFunctionType.Copy
+ADD = mybir.AluOpType.add
+MULT = mybir.AluOpType.mult
+MAX = mybir.AluOpType.max
+
+P = 128
+PACK = 4
+HALF = S // 2
+WIDE = 2 * S
+
+
+def tile_picked_cdhpathbsum_none_p_kernel(
+    tc, x_words, x_scales, w1, gs, offs, n1, n2, ca, hc, n3, n4, n5, n6, out
+):
+    nc = tc.nc
+    with ExitStack() as ctx:
+        lists = ctx.enter_context(tc.tile_pool(name="lists", bufs=1))
+        sb = ctx.enter_context(tc.tile_pool(name="sb", bufs=1))
+        psum = ctx.enter_context(tc.psum_pool(name="psum", bufs=8))
+
+        def load_list(name, src):
+            held = lists.tile(list(src.shape), U16, name=name)
+            nc.sync.dma_start(held[:], src)
+            return held
+
+        def tile(name, shape, dtype, tag=None):
+            return sb.tile(shape, dtype, name=name, tag=tag or name, align_bytes=64)
+
+        def deal(dst, src):
+            nc.vector.tensor_copy(
+                dst[:].rearrange("p (t m) -> p m t", t=PACK), src[:].rearrange("p (m t) -> p m t", t=PACK)
+            )
+
+        def product(cols, stat_words, stat_scales, mov_words, mov_scales):
+            acc = psum.tile([P, cols], F32, name="acc")
+            nc.tensor.matmul_mx(
+                out=acc[:], lhsT=stat_words.bitcast(FP8X4), lhsT_scale=stat_scales,
+                rhs=mov_words.bitcast(FP8X4), rhs_scale=mov_scales, start=True, stop=True,
+            )
+            return acc
+
+        gain = tile("gain", [P, PACK], F32)
+        nc.scalar.dma_start(gain[:], gs.rearrange("(p t) o -> p (t o)", t=PACK))
+        w_rows = w1.rearrange("(p j) h -> p j h", j=PACK)
+        w_raw = []
+        for u in range(2):
+            raw = tile("w_raw%d" % u, [P, PACK, H // 2], F32)
+            nc.scalar.dma_start(raw[:], w_rows[:, :, u * (H // 2) : (u + 1) * (H // 2)])
+            w_raw.append(raw)
+        table = tile("table", [P, T], U32)
+        nc.scalar.dma_start(table[:].bitcast(I32), x_words[0].rearrange("p n j -> p (n j)").bitcast(I32))
+
+        offs_t = load_list("offs", offs)
+        plane = tile("plane", [P, T], U8)
+        for q in range(4):
+            rows = x_scales[0, 4 * q : 4 * q + 4, :].bitcast(I32)
+            nc.sync.dma_start(plane[32 * q : 32 * q + 32, :].bitcast(I32), rows.partition_broadcast(8))
+        ca_t = load_list("ca", ca)
+        hc_t = load_list("hc", hc)
+        n1_t = load_list("n1", n1)
+        n2_t = load_list("n2", n2)
+        n3_t = load_list("n3", n3)
+        n4_t = load_list("n4", n4)
+        n5_t = load_list("n5", n5)
+        n6_t = load_list("n6", n6)
+
+        hc_scales = tile("hc_scales", [P, C], U8)
+        nc.vector.memset(hc_scales[:].bitcast(I32), 0)
+
+        xq_scales = tile("xq_scales", [P, S], U8)
+        nc.vector.tensor_copy(xq_scales[:], plane[:].indirect(offs_t[:]))
+        ca_bytes = tile("ca_bytes", [P, C], U8)
+        nc.vector.tensor_copy(ca_bytes[:], plane[:].indirect(ca_t[:]))
+        hc_bytes = tile("hc_bytes", [P, C], U8)
+        nc.vector.tensor_copy(hc_bytes[:], plane[:].indirect(hc_t[:]))
+
+        M2 = P // 2
+        w_words = [tile("w_words%d" % t, [P, P], U32) for t in range(PACK)]
+        w_scales = [tile("w_scales%d" % t, [P, P], U8) for t in range(PACK)]
+        for u in range(2):
+            w_bf = tile("w_bf%d" % u, [P, PACK, M2 * PACK], BF16)
+            dst = w_bf[:].rearrange("p t (m j) -> p m j t", j=PACK)
+            src = w_raw[u][:].rearrange("p j (m t) -> p m j t", t=PACK)
+            nc.scalar.copy(dst, src)
+            for t in range(PACK):
+                cols = slice(u * M2, (u + 1) * M2)
+                nc.vector.quantize_mx(out=w_words[t][:, cols].bitcast(FP8X4), scales=w_scales[t][:, cols], in_=w_bf[:, t, :])
+
+        xq_words = tile("xq_words", [P, S], U32)
+        nc.vector.tensor_copy(xq_words[:], table[:].indirect(offs_t[:]))
+
+        y_win = []
+        for t in range(PACK):
+            acc = product(S, w_words[t][:], w_scales[t][:], xq_words[:], xq_scales[:])
+            win = tile("y_win%d" % t, [P, S], F32)
+            nc.vector.tensor_scalar(win[:], acc[:], gain[:, t : t + 1], None, MULT)
+            y_win.append(win)
+
+        ca_picked = tile("ca_picked", [P, C], U32, tag="xq_words")
+        nc.vector.tensor_copy(ca_picked[:], table[:].indirect(ca_t[:]))
+        ca_words = tile("ca_words", [P, C], U32)
+        deal(ca_words, ca_picked)
+        ca_scales = tile("ca_scales", [P, C], U8, tag="xq_scales")
+        deal(ca_scales, ca_bytes)
+        hc_dealt = tile("hc_dealt", [P, C], U8, tag="w_scales3")
+        deal(hc_dealt, hc_bytes)
+        for i in range(4):
+            nc.sync.dma_start(hc_scales[i:P:32, :].bitcast(I32), hc_dealt[i + 16 * (i // 2) : P : 32, :].bitcast(I32))
+
+        z_words = tile("z_words", [P, S], U32)
+        z_scales = tile("z_scales", [P, S], U8)
+        a_win = [tile("a_win%d" % t, [P, WIDE], F32) for t in range(PACK)]
+        b_win = [tile("b_win%d" % t, [P, WIDE], F32) for t in range(PACK)]
+        for u in range(2):
+            cols = slice(u * HALF, (u + 1) * HALF)
+            entries = slice(u * HALF // 16, (u + 1) * HALF // 16)
+            y1 = tile("y1_%d" % u, [P, PACK, HALF], F32)
+            y2 = tile("y2_%d" % u, [P, PACK, HALF], F32)
+            for t in range(PACK):
+                nc.scalar.activation(y1[:, t, :], y_win[t][:].indirect(n1_t[:, entries]), COPY)
+                nc.scalar.activation(y2[:, t, :], y_win[t][:].indirect(n2_t[:, entries]), COPY, scale=0.75)
+            z_bf = tile("z_bf%d" % u, [P, HALF * PACK], BF16)
+            nc.vector.tensor_tensor(
+                z_bf[:].rearrange("p (c i t) -> p c t i", i=4, t=PACK),
+                y1[:].rearrange("p t (c i) -> p c t i", i=4),
+                y2[:].rearrange("p t (c i) -> p c t i", i=4),
+                ADD,
+            )
+            nc.vector.quantize_mx(out=z_words[:, cols].bitcast(FP8X4), scales=z_scales[:, cols], in_=z_bf[:])
+            acc = product(HALF, ca_words[:, 0:P], ca_scales[:, 0:P], z_words[:, cols], z_scales[:, cols])
+            if u == 0:
+                nc.vector.tensor_scalar(a_win[0][:, cols], acc[:], 0.0625, None, MULT)
+            else:
+                nc.scalar.activation(a_win[0][:, cols], acc[:], COPY, scale=0.0625)
+
+        hc_picked = tile("hc_picked", [P, C], U32, tag="z_bf1")
+        nc.vector.tensor_copy(hc_picked[:], table[:].indirect(hc_t[:]))
+        hc_words = tile("hc_words", [P, C], U32)
+        deal(hc_words, hc_picked)
+
+        def scores(win, words, scales, t):
+            rows = slice(t * P, (t + 1) * P)
+            acc = product(S, words[:, rows], scales[:, rows], z_words[:], z_scales[:])
+            nc.vector.tensor_scalar(win[:, 0:S], acc[:], 0.0625, None, MULT)
+
+        def fetch(name, win, index):
+            got = tile(name, [P, S], F32)
+            nc.scalar.activation(got[:], win[:].indirect(index[:]), COPY)
+            return got
+
+        out_rows = out.rearrange("(p t) j -> p t j", t=PACK)
+        a3, a4 = {}, {}
+
+        def a_side(t):
+            if t > 0:
+                scores(a_win[t], ca_words, ca_scales, t)
+            a3[t] = fetch("a3_%d" % t, a_win[t], n3_t)
+            a4[t] = fetch("a4_%d" % t, a_win[t], n4_t)
+
+        def b_side(t):
+            scores(b_win[t], hc_words, hc_scales, t)
+            b5 = fetch("b5_%d" % t, b_win[t], n5_t)
+            first = tile("first%d" % t, [P, S], F32)
+            nc.vector.tensor_tensor(first[:], a3[t][:], b5[:], ADD)
+            b6 = fetch("b6_%d" % t, b_win[t], n6_t)
+            second = tile("second%d" % t, [P, S], F32)
+            nc.vector.tensor_tensor(second[:], a4[t][:], b6[:], ADD)
+            best = tile("best%d" % t, [P, S], F32)
+            nc.vector.tensor_tensor(best[:], first[:], second[:], MAX)
+            nc.sync.dma_start(out_rows[:, t, :], best[:])
+
+        a_side(0)
+        a_side(1)
+        a_side(2)
+        b_side(0)
+        a_side(3)
+        b_side(1)
+        b_side(2)
+        b_side(3)

@@ -40,9 +40,10 @@ def tile_picked_cdhpathbsum_none_p_kernel(
         def tile(name, shape, dtype, tag=None):
             return sb.tile(shape, dtype, name=name, tag=tag or name, align_bytes=64)
 
-        def deal(dst, src):
+        def deal(dst, src, run):
             nc.vector.tensor_copy(
-                dst[:].rearrange("p (t m) -> p m t", t=PACK), src[:].rearrange("p (m t) -> p m t", t=PACK)
+                dst[:].rearrange("p (t m i) -> p m t i", t=PACK, i=run),
+                src[:].rearrange("p (m i t) -> p m t i", t=PACK, i=run),
             )
 
         def product(cols, stat_words, stat_scales, mov_words, mov_scales):
@@ -53,26 +54,31 @@ def tile_picked_cdhpathbsum_none_p_kernel(
             )
             return acc
 
-        gain = tile("gain", [P, PACK], F32)
-        nc.scalar.dma_start(gain[:], gs.rearrange("(p t) o -> p (t o)", t=PACK))
+        plane = tile("plane", [P, T], U8)
+
+        def load_scale_rows(queue, q):
+            rows = x_scales[0, 4 * q : 4 * q + 4, :].bitcast(I32)
+            queue.dma_start(plane[32 * q : 32 * q + 32, :].bitcast(I32), rows.partition_broadcast(8))
+
+        load_scale_rows(nc.scalar, 3)
         w_rows = w1.rearrange("(p j) h -> p j h", j=PACK)
         w_raw = []
         for u in range(2):
             raw = tile("w_raw%d" % u, [P, PACK, H // 2], F32)
             nc.scalar.dma_start(raw[:], w_rows[:, :, u * (H // 2) : (u + 1) * (H // 2)])
             w_raw.append(raw)
-        table = tile("table", [P, T], U32)
-        nc.scalar.dma_start(table[:].bitcast(I32), x_words[0].rearrange("p n j -> p (n j)").bitcast(I32))
 
         offs_t = load_list("offs", offs)
-        plane = tile("plane", [P, T], U8)
-        for q in range(4):
-            rows = x_scales[0, 4 * q : 4 * q + 4, :].bitcast(I32)
-            nc.sync.dma_start(plane[32 * q : 32 * q + 32, :].bitcast(I32), rows.partition_broadcast(8))
         ca_t = load_list("ca", ca)
-        hc_t = load_list("hc", hc)
+        for q in range(3):
+            load_scale_rows(nc.sync, q)
+        table = tile("table", [P, T], U32)
+        nc.sync.dma_start(table[:].bitcast(I32), x_words[0].rearrange("p n j -> p (n j)").bitcast(I32))
+        gain = tile("gain", [P, PACK], F32)
+        nc.sync.dma_start(gain[:], gs.rearrange("(p t) o -> p (t o)", t=PACK))
         n1_t = load_list("n1", n1)
         n2_t = load_list("n2", n2)
+        hc_t = load_list("hc", hc)
         n3_t = load_list("n3", n3)
         n4_t = load_list("n4", n4)
         n5_t = load_list("n5", n5)
@@ -85,16 +91,16 @@ def tile_picked_cdhpathbsum_none_p_kernel(
         nc.vector.tensor_copy(xq_scales[:], plane[:].indirect(offs_t[:]))
         ca_bytes = tile("ca_bytes", [P, C], U8)
         nc.vector.tensor_copy(ca_bytes[:], plane[:].indirect(ca_t[:]))
-        hc_bytes = tile("hc_bytes", [P, C], U8)
-        nc.vector.tensor_copy(hc_bytes[:], plane[:].indirect(hc_t[:]))
+        ca_scales = tile("ca_scales", [P, C], U8)
+        deal(ca_scales, ca_bytes, 16)
 
         M2 = P // 2
         w_words = [tile("w_words%d" % t, [P, P], U32) for t in range(PACK)]
         w_scales = [tile("w_scales%d" % t, [P, P], U8) for t in range(PACK)]
         for u in range(2):
             w_bf = tile("w_bf%d" % u, [P, PACK, M2 * PACK], BF16)
-            dst = w_bf[:].rearrange("p t (m j) -> p m j t", j=PACK)
-            src = w_raw[u][:].rearrange("p j (m t) -> p m j t", t=PACK)
+            dst = w_bf[:].rearrange("p t (m j) -> p m t j", j=PACK)
+            src = w_raw[u][:].rearrange("p j (m t) -> p m t j", t=PACK)
             nc.scalar.copy(dst, src)
             for t in range(PACK):
                 cols = slice(u * M2, (u + 1) * M2)
@@ -113,13 +119,7 @@ def tile_picked_cdhpathbsum_none_p_kernel(
         ca_picked = tile("ca_picked", [P, C], U32, tag="xq_words")
         nc.vector.tensor_copy(ca_picked[:], table[:].indirect(ca_t[:]))
         ca_words = tile("ca_words", [P, C], U32)
-        deal(ca_words, ca_picked)
-        ca_scales = tile("ca_scales", [P, C], U8, tag="xq_scales")
-        deal(ca_scales, ca_bytes)
-        hc_dealt = tile("hc_dealt", [P, C], U8, tag="w_scales3")
-        deal(hc_dealt, hc_bytes)
-        for i in range(4):
-            nc.sync.dma_start(hc_scales[i:P:32, :].bitcast(I32), hc_dealt[i + 16 * (i // 2) : P : 32, :].bitcast(I32))
+        deal(ca_words, ca_picked, 4)
 
         z_words = tile("z_words", [P, S], U32)
         z_scales = tile("z_scales", [P, S], U8)
@@ -130,16 +130,19 @@ def tile_picked_cdhpathbsum_none_p_kernel(
             entries = slice(u * HALF // 16, (u + 1) * HALF // 16)
             y1 = tile("y1_%d" % u, [P, PACK, HALF], F32)
             y2 = tile("y2_%d" % u, [P, PACK, HALF], F32)
+            z_bf = tile("z_bf%d" % u, [P, HALF * PACK], BF16, tag="z_bf")
+            z_woven = z_bf[:].rearrange("p (n t) -> p n t", t=PACK)
             for t in range(PACK):
                 nc.scalar.activation(y1[:, t, :], y_win[t][:].indirect(n1_t[:, entries]), COPY)
                 nc.scalar.activation(y2[:, t, :], y_win[t][:].indirect(n2_t[:, entries]), COPY, scale=0.75)
-            z_bf = tile("z_bf%d" % u, [P, HALF * PACK], BF16)
-            nc.vector.tensor_tensor(
-                z_bf[:].rearrange("p (c i t) -> p c t i", i=4, t=PACK),
-                y1[:].rearrange("p t (c i) -> p c t i", i=4),
-                y2[:].rearrange("p t (c i) -> p c t i", i=4),
-                ADD,
-            )
+                if t % 2 == 1:
+                    pair = slice(t - 1, t + 1)
+                    nc.vector.tensor_tensor(
+                        z_woven[:, :, pair],
+                        y1[:, pair, :].rearrange("p t n -> p n t"),
+                        y2[:, pair, :].rearrange("p t n -> p n t"),
+                        ADD,
+                    )
             nc.vector.quantize_mx(out=z_words[:, cols].bitcast(FP8X4), scales=z_scales[:, cols], in_=z_bf[:])
             acc = product(HALF, ca_words[:, 0:P], ca_scales[:, 0:P], z_words[:, cols], z_scales[:, cols])
             if u == 0:
@@ -147,10 +150,12 @@ def tile_picked_cdhpathbsum_none_p_kernel(
             else:
                 nc.scalar.activation(a_win[0][:, cols], acc[:], COPY, scale=0.0625)
 
-        hc_picked = tile("hc_picked", [P, C], U32, tag="z_bf1")
-        nc.vector.tensor_copy(hc_picked[:], table[:].indirect(hc_t[:]))
-        hc_words = tile("hc_words", [P, C], U32)
-        deal(hc_words, hc_picked)
+        hc_bytes = tile("hc_bytes", [P, C], U8, tag="z_bf")
+        nc.vector.tensor_copy(hc_bytes[:], plane[:].indirect(hc_t[:]))
+        hc_dealt = tile("hc_dealt", [P, C], U8)
+        deal(hc_dealt, hc_bytes, 16)
+        for i in range(4):
+            nc.sync.dma_start(hc_scales[i:P:32, :].bitcast(I32), hc_dealt[i + 16 * (i // 2) : P : 32, :].bitcast(I32))
 
         def scores(win, words, scales, t):
             rows = slice(t * P, (t + 1) * P)
@@ -158,36 +163,36 @@ def tile_picked_cdhpathbsum_none_p_kernel(
             nc.vector.tensor_scalar(win[:, 0:S], acc[:], 0.0625, None, MULT)
 
         def fetch(name, win, index):
-            got = tile(name, [P, S], F32)
-            nc.scalar.activation(got[:], win[:].indirect(index[:]), COPY)
+            got = tile(name, [P, 16 * index.shape[1]], F32)
+            nc.scalar.activation(got[:], win[:].indirect(index), COPY)
             return got
 
         out_rows = out.rearrange("(p t) j -> p t j", t=PACK)
-        a3, a4 = {}, {}
+        for t in range(1, PACK):
+            scores(a_win[t], ca_words, ca_scales, t)
+        a3, a4 = [], []
+        for t in range(PACK):
+            a3.append(fetch("a3_%d" % t, a_win[t], n3_t[:]))
+            a4.append(fetch("a4_%d" % t, a_win[t], n4_t[:]))
 
-        def a_side(t):
-            if t > 0:
-                scores(a_win[t], ca_words, ca_scales, t)
-            a3[t] = fetch("a3_%d" % t, a_win[t], n3_t)
-            a4[t] = fetch("a4_%d" % t, a_win[t], n4_t)
-
-        def b_side(t):
+        hc_picked = tile("hc_picked", [P, C], U32, tag="a_win0")
+        nc.vector.tensor_copy(hc_picked[:], table[:].indirect(hc_t[:]))
+        hc_words = tile("hc_words", [P, C], U32)
+        deal(hc_words, hc_picked, 4)
+        for t in range(PACK):
             scores(b_win[t], hc_words, hc_scales, t)
-            b5 = fetch("b5_%d" % t, b_win[t], n5_t)
+
+        for t in range(PACK):
+            b5 = fetch("b5_%d" % t, b_win[t], n5_t[:])
             first = tile("first%d" % t, [P, S], F32)
             nc.vector.tensor_tensor(first[:], a3[t][:], b5[:], ADD)
-            b6 = fetch("b6_%d" % t, b_win[t], n6_t)
-            second = tile("second%d" % t, [P, S], F32)
-            nc.vector.tensor_tensor(second[:], a4[t][:], b6[:], ADD)
-            best = tile("best%d" % t, [P, S], F32)
-            nc.vector.tensor_tensor(best[:], first[:], second[:], MAX)
-            nc.sync.dma_start(out_rows[:, t, :], best[:])
-
-        a_side(0)
-        a_side(1)
-        a_side(2)
-        b_side(0)
-        a_side(3)
-        b_side(1)
-        b_side(2)
-        b_side(3)
+            pieces = 2 if t == PACK - 1 else 1
+            width = S // pieces
+            for u in range(pieces):
+                cols = slice(u * width, (u + 1) * width)
+                b6 = fetch("b6_%d_%d" % (t, u), b_win[t], n6_t[:, u * width // 16 : (u + 1) * width // 16])
+                second = tile("second%d_%d" % (t, u), [P, width], F32)
+                nc.vector.tensor_tensor(second[:], a4[t][:, cols], b6[:], ADD)
+                best = tile("best%d_%d" % (t, u), [P, width], F32)
+                nc.vector.tensor_tensor(best[:], first[:, cols], second[:], MAX)
+                nc.sync.dma_start(out_rows[:, t, cols], best[:])

@@ -56,29 +56,24 @@ def tile_picked_cdhpathbsum_none_p_kernel(
 
         plane = tile("plane", [P, T], U8)
 
-        def load_scale_rows(queue, q):
-            rows = x_scales[0, 4 * q : 4 * q + 4, :].bitcast(I32)
-            queue.dma_start(plane[32 * q : 32 * q + 32, :].bitcast(I32), rows.partition_broadcast(8))
-
-        load_scale_rows(nc.scalar, 3)
-        w_rows = w1.rearrange("(p j) h -> p j h", j=PACK)
-        w_raw = []
-        for u in range(2):
-            raw = tile("w_raw%d" % u, [P, PACK, H // 2], F32)
-            nc.scalar.dma_start(raw[:], w_rows[:, :, u * (H // 2) : (u + 1) * (H // 2)])
-            w_raw.append(raw)
-
         offs_t = load_list("offs", offs)
+        gain = tile("gain", [P, PACK], F32)
+        nc.scalar.dma_start(gain[:], gs.rearrange("(p t) o -> p (t o)", t=PACK))
+        w_raw = tile("w_raw", [P, PACK, H], F32)
+        nc.scalar.dma_start(w_raw[:], w1.rearrange("(p j) h -> p j h", j=PACK))
+        nc.vector.memset(plane[:].bitcast(I32), 0)
+        for i in range(4):
+            rows = x_scales[0, i:16:4, :].bitcast(I32)
+            if i < 2:
+                nc.sync.dma_start(plane[i:P:32, :].bitcast(I32), rows)
+            else:
+                nc.sync.dma_start(plane[i:P:16, :].bitcast(I32), rows.unsqueeze(1).broadcast_to([4, 2, T // 4]))
         ca_t = load_list("ca", ca)
-        for q in range(3):
-            load_scale_rows(nc.sync, q)
+        hc_t = load_list("hc", hc)
         table = tile("table", [P, T], U32)
         nc.sync.dma_start(table[:].bitcast(I32), x_words[0].rearrange("p n j -> p (n j)").bitcast(I32))
-        gain = tile("gain", [P, PACK], F32)
-        nc.sync.dma_start(gain[:], gs.rearrange("(p t) o -> p (t o)", t=PACK))
         n1_t = load_list("n1", n1)
         n2_t = load_list("n2", n2)
-        hc_t = load_list("hc", hc)
         n3_t = load_list("n3", n3)
         n4_t = load_list("n4", n4)
         n5_t = load_list("n5", n5)
@@ -91,19 +86,16 @@ def tile_picked_cdhpathbsum_none_p_kernel(
         nc.vector.tensor_copy(xq_scales[:], plane[:].indirect(offs_t[:]))
         ca_bytes = tile("ca_bytes", [P, C], U8)
         nc.vector.tensor_copy(ca_bytes[:], plane[:].indirect(ca_t[:]))
-        ca_scales = tile("ca_scales", [P, C], U8)
-        deal(ca_scales, ca_bytes, 16)
 
         M2 = P // 2
         w_words = [tile("w_words%d" % t, [P, P], U32) for t in range(PACK)]
         w_scales = [tile("w_scales%d" % t, [P, P], U8) for t in range(PACK)]
+        w_view = w_raw[:].rearrange("p j (m t) -> p m t j", t=PACK)
         for u in range(2):
+            cols = slice(u * M2, (u + 1) * M2)
             w_bf = tile("w_bf%d" % u, [P, PACK, M2 * PACK], BF16)
-            dst = w_bf[:].rearrange("p t (m j) -> p m t j", j=PACK)
-            src = w_raw[u][:].rearrange("p j (m t) -> p m t j", t=PACK)
-            nc.scalar.copy(dst, src)
+            nc.scalar.copy(w_bf[:].rearrange("p t (m j) -> p m t j", j=PACK), w_view[:, cols, :, :])
             for t in range(PACK):
-                cols = slice(u * M2, (u + 1) * M2)
                 nc.vector.quantize_mx(out=w_words[t][:, cols].bitcast(FP8X4), scales=w_scales[t][:, cols], in_=w_bf[:, t, :])
 
         xq_words = tile("xq_words", [P, S], U32)
@@ -116,6 +108,8 @@ def tile_picked_cdhpathbsum_none_p_kernel(
             nc.vector.tensor_scalar(win[:], acc[:], gain[:, t : t + 1], None, MULT)
             y_win.append(win)
 
+        ca_scales = tile("ca_scales", [P, C], U8, tag="w_bf1")
+        deal(ca_scales, ca_bytes, 16)
         ca_picked = tile("ca_picked", [P, C], U32, tag="xq_words")
         nc.vector.tensor_copy(ca_picked[:], table[:].indirect(ca_t[:]))
         ca_words = tile("ca_words", [P, C], U32)
@@ -152,10 +146,6 @@ def tile_picked_cdhpathbsum_none_p_kernel(
 
         hc_bytes = tile("hc_bytes", [P, C], U8, tag="z_bf")
         nc.vector.tensor_copy(hc_bytes[:], plane[:].indirect(hc_t[:]))
-        hc_dealt = tile("hc_dealt", [P, C], U8)
-        deal(hc_dealt, hc_bytes, 16)
-        for i in range(4):
-            nc.sync.dma_start(hc_scales[i:P:32, :].bitcast(I32), hc_dealt[i + 16 * (i // 2) : P : 32, :].bitcast(I32))
 
         def scores(win, words, scales, t):
             rows = slice(t * P, (t + 1) * P)
@@ -170,6 +160,10 @@ def tile_picked_cdhpathbsum_none_p_kernel(
         out_rows = out.rearrange("(p t) j -> p t j", t=PACK)
         for t in range(1, PACK):
             scores(a_win[t], ca_words, ca_scales, t)
+        hc_dealt = tile("hc_dealt", [P, C], U8, tag="w_bf1")
+        deal(hc_dealt, hc_bytes, 16)
+        for i in range(4):
+            nc.sync.dma_start(hc_scales[i:P:32, :].bitcast(I32), hc_dealt[i + 16 * (i // 2) : P : 32, :].bitcast(I32))
         a3, a4 = [], []
         for t in range(PACK):
             a3.append(fetch("a3_%d" % t, a_win[t], n3_t[:]))

from contextlib import ExitStack

import concourse.mybir as mybir

K, T, S, H, C = 512, 2048, 256, 512, 512
FLOPS = 2 * K * H * S + 2 * 2 * K * C * S

F32 = mybir.dt.float32
BF16 = mybir.dt.bfloat16
I32 = mybir.dt.int32
U32 = mybir.dt.uint32
U16 = mybir.dt.uint16
U8 = mybir.dt.uint8
FP8X4 = mybir.dt.float8_e4m3fn_x4
COPY = mybir.ActivationFunctionType.Copy
ADD = mybir.AluOpType.add
MULT = mybir.AluOpType.mult
MAX = mybir.AluOpType.max

P = 128
PACK = 4
HALF = S // 2
WIDE = 2 * S


def tile_picked_cdhpathbsum_none_p_kernel(
    tc, x_words, x_scales, w1, gs, offs, n1, n2, ca, hc, n3, n4, n5, n6, out
):
    nc = tc.nc
    with ExitStack() as ctx:
        lists = ctx.enter_context(tc.tile_pool(name="lists", bufs=1))
        sb = ctx.enter_context(tc.tile_pool(name="sb", bufs=1))
        psum = ctx.enter_context(tc.psum_pool(name="psum", bufs=8))

        def load_list(name, src):
            held = lists.tile(list(src.shape), U16, name=name)
            nc.sync.dma_start(held[:], src)
            return held

        def tile(name, shape, dtype, tag=None):
            return sb.tile(shape, dtype, name=name, tag=tag or name, align_bytes=64)

        def deal(dst, src, run):
            nc.vector.tensor_copy(
                dst[:].rearrange("p (t m i) -> p m t i", t=PACK, i=run),
                src[:].rearrange("p (m i t) -> p m t i", t=PACK, i=run),
            )

        def product(cols, stat_words, stat_scales, mov_words, mov_scales):
            acc = psum.tile([P, cols], F32, name="acc")
            nc.tensor.matmul_mx(
                out=acc[:], lhsT=stat_words.bitcast(FP8X4), lhsT_scale=stat_scales,
                rhs=mov_words.bitcast(FP8X4), rhs_scale=mov_scales, start=True, stop=True,
            )
            return acc

        plane = tile("plane", [P, T], U8)

        offs_t = load_list("offs", offs)
        gain = tile("gain", [P, PACK], F32)
        nc.scalar.dma_start(gain[:], gs.rearrange("(p t) o -> p (t o)", t=PACK))
        w_raw = tile("w_raw", [P, PACK, H], F32)
        nc.scalar.dma_start(w_raw[:], w1.rearrange("(p j) h -> p j h", j=PACK))
        nc.vector.memset(plane[:].bitcast(I32), 0)
        for i in range(4):
            rows = x_scales[0, i:16:4, :].bitcast(I32)
            if i < 2:
                nc.sync.dma_start(plane[i:P:32, :].bitcast(I32), rows)
            else:
                nc.sync.dma_start(plane[i:P:16, :].bitcast(I32), rows.unsqueeze(1).broadcast_to([4, 2, T // 4]))
        ca_t = load_list("ca", ca)
        hc_t = load_list("hc", hc)
        table = tile("table", [P, T], U32)
        nc.sync.dma_start(table[:].bitcast(I32), x_words[0].rearrange("p n j -> p (n j)").bitcast(I32))
        n1_t = load_list("n1", n1)
        n2_t = load_list("n2", n2)
        n3_t = load_list("n3", n3)
        n4_t = load_list("n4", n4)
        n5_t = load_list("n5", n5)
        n6_t = load_list("n6", n6)

        hc_scales = tile("hc_scales", [P, C], U8)
        nc.vector.memset(hc_scales[:].bitcast(I32), 0)

        xq_scales = tile("xq_scales", [P, S], U8)
        nc.vector.tensor_copy(xq_scales[:], plane[:].indirect(offs_t[:]))
        ca_bytes = tile("ca_bytes", [P, C], U8)
        nc.vector.tensor_copy(ca_bytes[:], plane[:].indirect(ca_t[:]))

        M2 = P // 2
        w_words = [tile("w_words%d" % t, [P, P], U32) for t in range(PACK)]
        w_scales = [tile("w_scales%d" % t, [P, P], U8) for t in range(PACK)]
        w_view = w_raw[:].rearrange("p j (m t) -> p m t j", t=PACK)
        for u in range(2):
            cols = slice(u * M2, (u + 1) * M2)
            w_bf = tile("w_bf%d" % u, [P, PACK, M2 * PACK], BF16)
            nc.scalar.copy(w_bf[:].rearrange("p t (m j) -> p m t j", j=PACK), w_view[:, cols, :, :])
            for t in range(PACK):
                nc.vector.quantize_mx(out=w_words[t][:, cols].bitcast(FP8X4), scales=w_scales[t][:, cols], in_=w_bf[:, t, :])

        xq_words = tile("xq_words", [P, S], U32)
        nc.vector.tensor_copy(xq_words[:], table[:].indirect(offs_t[:]))

        y_win = []
        for t in range(PACK):
            acc = product(S, w_words[t][:], w_scales[t][:], xq_words[:], xq_scales[:])
            win = tile("y_win%d" % t, [P, S], F32)
            nc.vector.tensor_scalar(win[:], acc[:], gain[:, t : t + 1], None, MULT)
            y_win.append(win)

        ca_scales = tile("ca_scales", [P, C], U8, tag="w_bf1")
        deal(ca_scales, ca_bytes, 16)
        ca_picked = tile("ca_picked", [P, C], U32, tag="xq_words")
        nc.vector.tensor_copy(ca_picked[:], table[:].indirect(ca_t[:]))
        ca_words = tile("ca_words", [P, C], U32)
        deal(ca_words, ca_picked, 4)

        z_words = tile("z_words", [P, S], U32)
        z_scales = tile("z_scales", [P, S], U8)
        a_win = [tile("a_win%d" % t, [P, WIDE], F32) for t in range(PACK)]
        b_win = [tile("b_win%d" % t, [P, WIDE], F32) for t in range(PACK)]
        for u in range(2):
            cols = slice(u * HALF, (u + 1) * HALF)
            entries = slice(u * HALF // 16, (u + 1) * HALF // 16)
            y1 = tile("y1_%d" % u, [P, PACK, HALF], F32)
            y2 = tile("y2_%d" % u, [P, PACK, HALF], F32)
            z_bf = tile("z_bf%d" % u, [P, HALF * PACK], BF16, tag="z_bf")
            z_woven = z_bf[:].rearrange("p (n t) -> p n t", t=PACK)
            for t in range(PACK):
                nc.scalar.activation(y1[:, t, :], y_win[t][:].indirect(n1_t[:, entries]), COPY)
                nc.scalar.activation(y2[:, t, :], y_win[t][:].indirect(n2_t[:, entries]), COPY, scale=0.75)
                if t % 2 == 1:
                    pair = slice(t - 1, t + 1)
                    nc.vector.tensor_tensor(
                        z_woven[:, :, pair],
                        y1[:, pair, :].rearrange("p t n -> p n t"),
                        y2[:, pair, :].rearrange("p t n -> p n t"),
                        ADD,
                    )
            nc.vector.quantize_mx(out=z_words[:, cols].bitcast(FP8X4), scales=z_scales[:, cols], in_=z_bf[:])
            acc = product(HALF, ca_words[:, 0:P], ca_scales[:, 0:P], z_words[:, cols], z_scales[:, cols])
            if u == 0:
                nc.vector.tensor_scalar(a_win[0][:, cols], acc[:], 0.0625, None, MULT)
            else:
                nc.scalar.activation(a_win[0][:, cols], acc[:], COPY, scale=0.0625)

        hc_bytes = tile("hc_bytes", [P, C], U8, tag="z_bf")
        nc.vector.tensor_copy(hc_bytes[:], plane[:].indirect(hc_t[:]))

        def scores(win, words, scales, t):
            rows = slice(t * P, (t + 1) * P)
            acc = product(S, words[:, rows], scales[:, rows], z_words[:], z_scales[:])
            nc.vector.tensor_scalar(win[:, 0:S], acc[:], 0.0625, None, MULT)

        def fetch(name, win, index):
            got = tile(name, [P, 16 * index.shape[1]], F32)
            nc.scalar.activation(got[:], win[:].indirect(index), COPY)
            return got

        out_rows = out.rearrange("(p t) j -> p t j", t=PACK)
        for t in range(1, PACK):
            scores(a_win[t], ca_words, ca_scales, t)
        hc_dealt = tile("hc_dealt", [P, C], U8, tag="w_bf1")
        deal(hc_dealt, hc_bytes, 16)
        for i in range(4):
            nc.sync.dma_start(hc_scales[i:P:32, :].bitcast(I32), hc_dealt[i + 16 * (i // 2) : P : 32, :].bitcast(I32))
        a3, a4 = [], []
        for t in range(PACK):
            a3.append(fetch("a3_%d" % t, a_win[t], n3_t[:]))
            a4.append(fetch("a4_%d" % t, a_win[t], n4_t[:]))

        hc_picked = tile("hc_picked", [P, C], U32, tag="a_win0")
        nc.vector.tensor_copy(hc_picked[:], table[:].indirect(hc_t[:]))
        hc_words = tile("hc_words", [P, C], U32)
        deal(hc_words, hc_picked, 4)
        for t in range(PACK):
            scores(b_win[t], hc_words, hc_scales, t)

        for t in range(PACK):
            b5 = fetch("b5_%d" % t, b_win[t], n5_t[:])
            first = tile("first%d" % t, [P, S], F32)
            nc.vector.tensor_tensor(first[:], a3[t][:], b5[:], ADD)
            pieces = 2 if t == PACK - 1 else 1
            width = S // pieces
            for u in range(pieces):
                cols = slice(u * width, (u + 1) * width)
                b6 = fetch("b6_%d_%d" % (t, u), b_win[t], n6_t[:, u * width // 16 : (u + 1) * width // 16])
                second = tile("second%d_%d" % (t, u), [P, width], F32)
                nc.vector.tensor_tensor(second[:], a4[t][:, cols], b6[:], ADD)
                best = tile("best%d_%d" % (t, u), [P, width], F32)
                nc.vector.tensor_tensor(best[:], first[:, cols], second[:], MAX)
                nc.sync.dma_start(out_rows[:, t, cols], best[:])
